import numpy as np
import ml_dtypes


def mxq(x, axis, fmt="e4m3"):
    dtype, down = {"e4m3": (ml_dtypes.float8_e4m3fn, 7), "e5m2": (ml_dtypes.float8_e5m2, 14)}[fmt]
    v = np.moveaxis(np.asarray(x, np.float32).astype(ml_dtypes.bfloat16).astype(np.float64), axis, -1)
    blocks = v.reshape(v.shape[:-1] + (-1, 32))
    amax = np.abs(blocks).max(-1, keepdims=True)
    byte = np.maximum(np.where(amax > 0, np.frexp(amax)[1] - 1 + 127, 0) - down, 1)
    scale = np.exp2(byte - 127.0)
    codes = (blocks / scale).astype(np.float32).astype(dtype).astype(np.float64)
    return np.moveaxis((codes * scale).reshape(v.shape), -1, axis)


WIDE = False


def mx_kscale(k):
    if not WIDE:
        return np.ones(k)
    levels = np.array([30, -30])
    if k % 512:
        return np.exp2(np.random.permutation(np.resize(levels, k // 32))).repeat(32)
    a = np.empty((k // 512, 16))
    for p in range(k // 512):
        a[p, :8] = np.random.permutation(np.resize(levels, 8))
        for g in range(8):
            far = levels[np.abs(levels - a[p, g]) >= 10]
            a[p, g + 8] = far[np.random.randint(len(far))]
    return np.exp2(a.ravel()).repeat(32)


def f64(x):
    return np.asarray(x).astype(np.float64)


def striped8(idx):
    return np.asarray(idx).reshape(8, -1, 16).transpose(0, 2, 1).reshape(128, -1).astype(np.uint16)


def unstriped8(offs):
    return offs.reshape(8, 16, -1).transpose(0, 2, 1).reshape(8, -1).astype(np.int64)


def pick8(x, idx, run):
    r = np.arange(len(x))
    return x[r[:, None], idx[r % (8 * run) // run]]


E2M1 = np.array([0.0, 0.5, 1.0, 1.5, 2.0, 3.0, 4.0, 6.0, -0.0, -0.5, -1.0, -1.5, -2.0, -3.0, -4.0, -6.0])


def pack_weight(w, fmt):
    k, n = w.shape
    w = f64(np.asarray(w, np.float32).astype(ml_dtypes.bfloat16)).reshape(k // 32, 32, n)
    amax = np.abs(w).max(1)
    if fmt == "e4m3":
        byte = np.frexp(amax)[1] - 1 + 127 - 7
    else:
        mant, ex = np.frexp(amax / 6.0)
        byte = np.where(mant > 0.5, ex, ex - 1) + 127
    byte = np.clip(np.where(amax > 0, byte, 1), 1, 254)
    scaled = (w * np.exp2(127.0 - byte)[:, None, :]).reshape(k, n).astype(np.float32)
    by_word = np.ascontiguousarray(scaled.reshape(k // 512, 128, 4, n).transpose(0, 1, 3, 2))
    if fmt == "e4m3":
        words = by_word.astype(ml_dtypes.float8_e4m3fn).view(np.uint8)
    else:
        c = by_word.astype(ml_dtypes.float4_e2m1fn).view(np.uint8) & 0xF
        words = (c[..., 0::2] | (c[..., 1::2] << 4)).reshape(k // 512, 128, 2 * n)
    return np.ascontiguousarray(words), np.ascontiguousarray(byte.astype(np.uint8).reshape(k // 512, 16, n))


def unpack_weight(words, scales, fmt):
    g, _, n = scales.shape
    words = np.ascontiguousarray(words).reshape(g, 128, n, -1)
    if fmt == "e4m3":
        vals = words.view(ml_dtypes.float8_e4m3fn).astype(np.float64)
    else:
        nib = np.empty((g, 128, n, 4), np.uint8)
        nib[..., 0::2] = words & 0xF
        nib[..., 1::2] = words >> 4
        vals = E2M1[nib]
    vals = vals * np.repeat(np.exp2(scales.astype(np.float64) - 127.0), 8, axis=1)[..., None]
    return vals.transpose(0, 1, 3, 2).reshape(g * 512, n)


N, K, T, J = 512, 512, 1024, 512


def setup_inputs():
    n = np.random.standard_normal
    idx = np.stack([np.random.permutation(T)[:J] for _ in range(8)])
    fn = mx_kscale(N)
    wp = pack_weight(n((N, K)) * 1 / np.sqrt(N) * fn[:, None], "e2m1")
    return {
        "g": (n((N, T)) * np.exp(0.5 * n((1, T))) / fn[:, None]).astype(np.float32),
        "gm": (np.random.uniform(0.5, 2.0, (N, 1))).astype(np.float32),
        "w_words": wp[0],
        "w_scales": wp[1],
        "base": (1.0 * n((K, J))).astype(np.float32),
        "offs": striped8(idx),
    }


def reference(g, gm, w_words, w_scales, base, offs):
    idx = unstriped8(offs)
    wu = unpack_weight(w_words, w_scales, "e2m1")
    d = pick8(f64(g), idx, 64) * f64(gm)
    dq = mxq(d, 0, "e5m2")
    dx = wu.T @ dq
    y = dx + 0.5 * f64(base)
    return y

@@ -1,0 +1,101 @@
+from contextlib import ExitStack
+
+import concourse.mybir as mybir
+
+N, K, T, J = 512, 512, 1024, 512
+FLOPS = 2 * N * K * J
+
+F32 = mybir.dt.float32
+BF16 = mybir.dt.bfloat16
+I32 = mybir.dt.int32
+U32 = mybir.dt.uint32
+U16 = mybir.dt.uint16
+U8 = mybir.dt.uint8
+E5M2X4 = mybir.dt.float8_e5m2_x4
+E2M1X4 = mybir.dt.float4_e2m1fn_x4
+COPY = mybir.ActivationFunctionType.Copy
+MULT = mybir.AluOpType.mult
+ADD = mybir.AluOpType.add
+
+P = 128
+PACK = 4
+HALF = J // 2
+
+
+def tile_list_head_token_grads_kernel(tc, g, gm, w_words, w_scales, base, offs, out):
+    nc = tc.nc
+    with ExitStack() as ctx:
+        keep = ctx.enter_context(tc.tile_pool(name="keep", bufs=1))
+        psum = ctx.enter_context(tc.psum_pool(name="psum", bufs=1))
+
+        offsets = keep.tile([P, J // 16], U16, name="offsets")
+        nc.sync.dma_start(offsets[:], offs)
+
+        g_rows = g.rearrange("(p t) c -> p t c", t=PACK)
+        planes = []
+        for t in range(PACK):
+            plane = keep.tile([P, T], F32, name="plane%d" % t)
+            nc.sync.dma_start(plane[:], g_rows[:, t, :])
+            planes.append(plane)
+        factor = keep.tile([P, PACK], F32, name="factor")
+        nc.scalar.dma_start(factor[:], gm.rearrange("(p t) o -> p (t o)", t=PACK))
+
+        w_codes = keep.tile([P, 2 * K], U8, name="w_codes", align_bytes=64)
+        nc.sync.dma_start(w_codes[:].bitcast(I32), w_words[0].bitcast(I32))
+        w_plane = keep.tile([P, K], U8, name="w_plane", align_bytes=64)
+        nc.gpsimd.memset(w_plane[:].bitcast(I32), 0)
+        for q in range(4):
+            nc.sync.dma_start(
+                w_plane[32 * q : 32 * q + 4, :].bitcast(I32),
+                w_scales[0, 4 * q : 4 * q + 4, :].bitcast(I32),
+            )
+        bases = []
+        for m in range(K // P):
+            base_sb = keep.tile([P, J], F32, name="base%d" % m)
+            nc.sync.dma_start(base_sb[:], base[m * P : (m + 1) * P, :])
+            bases.append(base_sb)
+
+        pairs = [keep.tile([P, PACK * HALF], BF16, name="pairs%d" % h, align_bytes=64) for h in range(2)]
+        slots = [pair[:].rearrange("p (u j e) -> p u j e", u=2, e=2) for pair in pairs]
+        for t in range(2):
+            picked = keep.tile([P, J], F32, name="picked%d" % t)
+            nc.vector.tensor_copy(picked[:], planes[t][:].indirect(offsets[:]))
+            for h in range(2):
+                nc.scalar.activation(
+                    slots[h][:, t // 2, :, t % 2], picked[:, h * HALF : (h + 1) * HALF], COPY, scale=factor[:, t : t + 1]
+                )
+        for t in range(2, PACK):
+            for h in range(2):
+                picked = keep.tile([P, HALF], F32, name="picked%d_%d" % (t, h))
+                nc.vector.tensor_copy(picked[:], planes[t][:].indirect(offsets[:, h * HALF // 16 : (h + 1) * HALF // 16]))
+                nc.scalar.activation(slots[h][:, t // 2, :, t % 2], picked[:], COPY, scale=factor[:, t : t + 1])
+
+        d_codes = keep.tile([P, J], U32, name="d_codes", align_bytes=64)
+        d_plane = keep.tile([P, J], U8, name="d_plane", align_bytes=64)
+        woven = [keep.tile([P, PACK * HALF], BF16, name="woven%d" % h, align_bytes=64) for h in range(2)]
+        for h in range(2):
+            nc.vector.tensor_copy(
+                woven[h][:].bitcast(I32).rearrange("p (j u) -> p j u", u=2),
+                pairs[h][:].bitcast(I32).rearrange("p (u j) -> p j u", u=2),
+            )
+        for h in range(2):
+            cols = slice(h * HALF, (h + 1) * HALF)
+            nc.vector.quantize_mx(out=d_codes[:, cols].bitcast(E5M2X4), scales=d_plane[:, cols], in_=woven[h][:])
+
+        for m in range(K // P):
+            acc = psum.tile([P, J], F32, name="acc%d" % m)
+            nc.tensor.matmul_mx(
+                out=acc[:],
+                lhsT=w_codes[:, 2 * P * m : 2 * P * (m + 1)].bitcast(E2M1X4),
+                lhsT_scale=w_plane[:, P * m : P * (m + 1)],
+                rhs=d_codes[:].bitcast(E5M2X4),
+                rhs_scale=d_plane[:],
+                start=True,
+                stop=True,
+            )
+            width = HALF if m == K // P - 1 else J
+            for c in range(0, J, width):
+                cols = slice(c, c + width)
+                result = keep.tile([P, width], F32, name="result%d_%d" % (m, c))
+                nc.vector.scalar_tensor_tensor(result[:], bases[m][:, cols], 0.5, acc[:, cols], MULT, ADD)
+                nc.sync.dma_start(out[m * P : (m + 1) * P, cols], result[:])

@@ -29,7 +29,9 @@ def tile_list_head_token_grads_kernel(tc, g, gm, w_words, w_scales, base, offs, 
         psum = ctx.enter_context(tc.psum_pool(name="psum", bufs=1))
 
         offsets = keep.tile([P, J // 16], U16, name="offsets")
-        nc.sync.dma_start(offsets[:], offs)
+        warm = keep.tile([P, 2], F32, name="warm")
+        nc.vector.memset(warm[:, 0:1], 0.0)
+        nc.scalar.activation(warm[:, 1:2], warm[:, 0:1], COPY)
 
         g_rows = g.rearrange("(p t) c -> p t c", t=PACK)
         planes = []
@@ -37,6 +39,8 @@ def tile_list_head_token_grads_kernel(tc, g, gm, w_words, w_scales, base, offs, 
             plane = keep.tile([P, T], F32, name="plane%d" % t)
             nc.sync.dma_start(plane[:], g_rows[:, t, :])
             planes.append(plane)
+            if t == 0:
+                nc.sync.dma_start(offsets[:], offs)
         factor = keep.tile([P, PACK], F32, name="factor")
         nc.scalar.dma_start(factor[:], gm.rearrange("(p t) o -> p (t o)", t=PACK))
 
@@ -45,15 +49,12 @@ def tile_list_head_token_grads_kernel(tc, g, gm, w_words, w_scales, base, offs, 
         w_plane = keep.tile([P, K], U8, name="w_plane", align_bytes=64)
         nc.gpsimd.memset(w_plane[:].bitcast(I32), 0)
         for q in range(4):
-            nc.sync.dma_start(
+            nc.gpsimd.dma_start(
                 w_plane[32 * q : 32 * q + 4, :].bitcast(I32),
                 w_scales[0, 4 * q : 4 * q + 4, :].bitcast(I32),
             )
-        bases = []
-        for m in range(K // P):
-            base_sb = keep.tile([P, J], F32, name="base%d" % m)
-            nc.sync.dma_start(base_sb[:], base[m * P : (m + 1) * P, :])
-            bases.append(base_sb)
+        base_sb = keep.tile([P, K // P, J], F32, name="base_sb")
+        nc.sync.dma_start(base_sb[:], base.rearrange("(m p) j -> p m j", p=P))
 
         pairs = [keep.tile([P, PACK * HALF], BF16, name="pairs%d" % h, align_bytes=64) for h in range(2)]
         slots = [pair[:].rearrange("p (u j e) -> p u j e", u=2, e=2) for pair in pairs]
@@ -97,5 +98,5 @@ def tile_list_head_token_grads_kernel(tc, g, gm, w_words, w_scales, base, offs, 
             for c in range(0, J, width):
                 cols = slice(c, c + width)
                 result = keep.tile([P, width], F32, name="result%d_%d" % (m, c))
-                nc.vector.scalar_tensor_tensor(result[:], bases[m][:, cols], 0.5, acc[:, cols], MULT, ADD)
+                nc.vector.scalar_tensor_tensor(result[:], base_sb[:, m, cols], 0.5, acc[:, cols], MULT, ADD)
                 nc.sync.dma_start(out[m * P : (m + 1) * P, cols], result[:])

@@ -20,6 +20,8 @@ ADD = mybir.AluOpType.add
 P = 128
 PACK = 4
 HALF = J // 2
+PIECE = 128
+PIECES = J // PIECE
 
 
 def tile_list_head_token_grads_kernel(tc, g, gm, w_words, w_scales, base, offs, out):
@@ -56,32 +58,35 @@ def tile_list_head_token_grads_kernel(tc, g, gm, w_words, w_scales, base, offs, 
         base_sb = keep.tile([P, K // P, J], F32, name="base_sb")
         nc.sync.dma_start(base_sb[:], base.rearrange("(m p) j -> p m j", p=P))
 
-        pairs = [keep.tile([P, PACK * HALF], BF16, name="pairs%d" % h, align_bytes=64) for h in range(2)]
-        slots = [pair[:].rearrange("p (u j e) -> p u j e", u=2, e=2) for pair in pairs]
-        for t in range(2):
-            picked = keep.tile([P, J], F32, name="picked%d" % t)
-            nc.vector.tensor_copy(picked[:], planes[t][:].indirect(offsets[:]))
-            for h in range(2):
-                nc.scalar.activation(
-                    slots[h][:, t // 2, :, t % 2], picked[:, h * HALF : (h + 1) * HALF], COPY, scale=factor[:, t : t + 1]
-                )
-        for t in range(2, PACK):
-            for h in range(2):
-                picked = keep.tile([P, HALF], F32, name="picked%d_%d" % (t, h))
-                nc.vector.tensor_copy(picked[:], planes[t][:].indirect(offsets[:, h * HALF // 16 : (h + 1) * HALF // 16]))
-                nc.scalar.activation(slots[h][:, t // 2, :, t % 2], picked[:], COPY, scale=factor[:, t : t + 1])
+        last_factor = keep.tile([P, PIECE], F32, name="last_factor")
+        nc.scalar.copy(last_factor[:], factor[:, PACK - 1 : PACK].to_broadcast([P, PIECE]))
+
+        scaled = [keep.tile([P, PACK, PIECE], F32, name="scaled%d" % q) for q in range(PIECES)]
+        for t in range(PACK - 1):
+            width = HALF if t == PACK - 2 else J
+            for first in range(0, J, width):
+                picked = keep.tile([P, width], F32, name="picked%d_%d" % (t, first))
+                nc.vector.tensor_copy(picked[:], planes[t][:].indirect(offsets[:, first // 16 : (first + width) // 16]))
+                for c in range(0, width, PIECE):
+                    nc.scalar.activation(
+                        scaled[(first + c) // PIECE][:, t, :], picked[:, c : c + PIECE], COPY, scale=factor[:, t : t + 1]
+                    )
+        for q in range(PIECES):
+            entries = offsets[:, q * PIECE // 16 : (q + 1) * PIECE // 16]
+            nc.vector.tensor_tensor(scaled[q][:, PACK - 1, :], planes[PACK - 1][:].indirect(entries), last_factor[:], MULT)
 
         d_codes = keep.tile([P, J], U32, name="d_codes", align_bytes=64)
         d_plane = keep.tile([P, J], U8, name="d_plane", align_bytes=64)
-        woven = [keep.tile([P, PACK * HALF], BF16, name="woven%d" % h, align_bytes=64) for h in range(2)]
-        for h in range(2):
-            nc.vector.tensor_copy(
-                woven[h][:].bitcast(I32).rearrange("p (j u) -> p j u", u=2),
-                pairs[h][:].bitcast(I32).rearrange("p (u j) -> p j u", u=2),
+        woven = [keep.tile([P, PACK * PIECE], BF16, name="woven%d" % q, align_bytes=64) for q in range(PIECES)]
+        for q in range(PIECES):
+            weave = nc.scalar.copy if q < PIECES // 2 else nc.vector.tensor_copy
+            weave(
+                woven[q][:].rearrange("p (c i t) -> p c t i", i=4, t=PACK),
+                scaled[q][:].rearrange("p t (c i) -> p c t i", i=4),
             )
-        for h in range(2):
-            cols = slice(h * HALF, (h + 1) * HALF)
-            nc.vector.quantize_mx(out=d_codes[:, cols].bitcast(E5M2X4), scales=d_plane[:, cols], in_=woven[h][:])
+        for q in (0, 2, 3, 1):
+            cols = slice(q * PIECE, (q + 1) * PIECE)
+            nc.vector.quantize_mx(out=d_codes[:, cols].bitcast(E5M2X4), scales=d_plane[:, cols], in_=woven[q][:])
 
         for m in range(K // P):
             acc = psum.tile([P, J], F32, name="acc%d" % m)

@@ -19,9 +19,17 @@ ADD = mybir.AluOpType.add
 
 P = 128
 PACK = 4
+LAST = PACK - 1
+PER_COLUMN = 16
+QUADRANT = 32
+SCALE_ROWS = 4
 HALF = J // 2
 PIECE = 128
 PIECES = J // PIECE
+RUN = 4
+BANKS = K // P
+
+PIECE_ORDER = list(range(0, PIECES, 2)) + list(range(1, PIECES, 2))
 
 
 def tile_list_head_token_grads_kernel(tc, g, gm, w_words, w_scales, base, offs, out):
@@ -30,7 +38,8 @@ def tile_list_head_token_grads_kernel(tc, g, gm, w_words, w_scales, base, offs, 
         keep = ctx.enter_context(tc.tile_pool(name="keep", bufs=1))
         psum = ctx.enter_context(tc.psum_pool(name="psum", bufs=1))
 
-        offsets = keep.tile([P, J // 16], U16, name="offsets")
+        offsets = keep.tile([P, J // PER_COLUMN], U16, name="offsets")
+
         warm = keep.tile([P, 2], F32, name="warm")
         nc.vector.memset(warm[:, 0:1], 0.0)
         nc.scalar.activation(warm[:, 1:2], warm[:, 0:1], COPY)
@@ -48,60 +57,62 @@ def tile_list_head_token_grads_kernel(tc, g, gm, w_words, w_scales, base, offs, 
 
         w_codes = keep.tile([P, 2 * K], U8, name="w_codes", align_bytes=64)
         nc.sync.dma_start(w_codes[:].bitcast(I32), w_words[0].bitcast(I32))
-        w_plane = keep.tile([P, K], U8, name="w_plane", align_bytes=64)
-        nc.gpsimd.memset(w_plane[:].bitcast(I32), 0)
-        for q in range(4):
-            nc.gpsimd.dma_start(
-                w_plane[32 * q : 32 * q + 4, :].bitcast(I32),
-                w_scales[0, 4 * q : 4 * q + 4, :].bitcast(I32),
+        w_scale_rows = keep.tile([P, K], U8, name="w_scale_rows", align_bytes=64)
+        nc.vector.memset(w_scale_rows[:].bitcast(I32), 0)
+        for quadrant in range(P // QUADRANT):
+            nc.sync.dma_start(
+                w_scale_rows[QUADRANT * quadrant : QUADRANT * quadrant + SCALE_ROWS, :].bitcast(I32),
+                w_scales[0, SCALE_ROWS * quadrant : SCALE_ROWS * (quadrant + 1), :].bitcast(I32),
             )
-        base_sb = keep.tile([P, K // P, J], F32, name="base_sb")
-        nc.sync.dma_start(base_sb[:], base.rearrange("(m p) j -> p m j", p=P))
+        base_rows = keep.tile([P, BANKS, J], F32, name="base_rows")
+        nc.sync.dma_start(base_rows[:], base.rearrange("(m p) j -> p m j", p=P))
 
         last_factor = keep.tile([P, PIECE], F32, name="last_factor")
-        nc.scalar.copy(last_factor[:], factor[:, PACK - 1 : PACK].to_broadcast([P, PIECE]))
+        nc.scalar.copy(last_factor[:], factor[:, LAST : LAST + 1].to_broadcast([P, PIECE]))
 
         scaled = [keep.tile([P, PACK, PIECE], F32, name="scaled%d" % q) for q in range(PIECES)]
-        for t in range(PACK - 1):
-            width = HALF if t == PACK - 2 else J
-            for first in range(0, J, width):
-                picked = keep.tile([P, width], F32, name="picked%d_%d" % (t, first))
-                nc.vector.tensor_copy(picked[:], planes[t][:].indirect(offsets[:, first // 16 : (first + width) // 16]))
-                for c in range(0, width, PIECE):
+        for t in range(LAST):
+            gathered = HALF if t == LAST - 1 else J
+            for first in range(0, J, gathered):
+                picked = keep.tile([P, gathered], F32, name="picked%d_%d" % (t, first))
+                entries = offsets[:, first // PER_COLUMN : (first + gathered) // PER_COLUMN]
+                nc.vector.tensor_copy(picked[:], planes[t][:].indirect(entries))
+                for c in range(0, gathered, PIECE):
                     nc.scalar.activation(
                         scaled[(first + c) // PIECE][:, t, :], picked[:, c : c + PIECE], COPY, scale=factor[:, t : t + 1]
                     )
-        for q in range(PIECES):
-            entries = offsets[:, q * PIECE // 16 : (q + 1) * PIECE // 16]
-            nc.vector.tensor_tensor(scaled[q][:, PACK - 1, :], planes[PACK - 1][:].indirect(entries), last_factor[:], MULT)
+        for q in PIECE_ORDER:
+            entries = offsets[:, q * PIECE // PER_COLUMN : (q + 1) * PIECE // PER_COLUMN]
+            nc.vector.tensor_tensor(scaled[q][:, LAST, :], planes[LAST][:].indirect(entries), last_factor[:], MULT)
 
         d_codes = keep.tile([P, J], U32, name="d_codes", align_bytes=64)
-        d_plane = keep.tile([P, J], U8, name="d_plane", align_bytes=64)
-        woven = [keep.tile([P, PACK * PIECE], BF16, name="woven%d" % q, align_bytes=64) for q in range(PIECES)]
-        for q in range(PIECES):
-            weave = nc.scalar.copy if q < PIECES // 2 else nc.vector.tensor_copy
+        d_scale_rows = keep.tile([P, J], U8, name="d_scale_rows", align_bytes=64)
+        woven = [keep.tile([P, PACK * HALF], BF16, name="woven%d" % h, align_bytes=64) for h in range(2)]
+        for q in PIECE_ORDER:
+            h, odd = divmod(q, 2)
+            weave = nc.vector.tensor_copy if odd else nc.scalar.copy
             weave(
-                woven[q][:].rearrange("p (c i t) -> p c t i", i=4, t=PACK),
-                scaled[q][:].rearrange("p t (c i) -> p c t i", i=4),
+                woven[h][:, PACK * PIECE * odd : PACK * PIECE * (odd + 1)].rearrange("p (c i t) -> p c t i", i=RUN, t=PACK),
+                scaled[q][:].rearrange("p t (c i) -> p c t i", i=RUN),
             )
-        for q in (0, 2, 3, 1):
-            cols = slice(q * PIECE, (q + 1) * PIECE)
-            nc.vector.quantize_mx(out=d_codes[:, cols].bitcast(E5M2X4), scales=d_plane[:, cols], in_=woven[q][:])
+        for h in range(2):
+            slots = slice(h * HALF, (h + 1) * HALF)
+            nc.vector.quantize_mx(out=d_codes[:, slots].bitcast(E5M2X4), scales=d_scale_rows[:, slots], in_=woven[h][:])
 
-        for m in range(K // P):
+        for m in range(BANKS):
             acc = psum.tile([P, J], F32, name="acc%d" % m)
             nc.tensor.matmul_mx(
                 out=acc[:],
                 lhsT=w_codes[:, 2 * P * m : 2 * P * (m + 1)].bitcast(E2M1X4),
-                lhsT_scale=w_plane[:, P * m : P * (m + 1)],
+                lhsT_scale=w_scale_rows[:, P * m : P * (m + 1)],
                 rhs=d_codes[:].bitcast(E5M2X4),
-                rhs_scale=d_plane[:],
+                rhs_scale=d_scale_rows[:],
                 start=True,
                 stop=True,
             )
-            width = HALF if m == K // P - 1 else J
-            for c in range(0, J, width):
-                cols = slice(c, c + width)
-                result = keep.tile([P, width], F32, name="result%d_%d" % (m, c))
-                nc.vector.scalar_tensor_tensor(result[:], base_sb[:, m, cols], 0.5, acc[:, cols], MULT, ADD)
-                nc.sync.dma_start(out[m * P : (m + 1) * P, cols], result[:])
+            stored = HALF if m == BANKS - 1 else J
+            for first in range(0, J, stored):
+                slots = slice(first, first + stored)
+                result = keep.tile([P, stored], F32, name="result%d_%d" % (m, first))
+                nc.vector.scalar_tensor_tensor(result[:], base_rows[:, m, slots], 0.5, acc[:, slots], MULT, ADD)
+                nc.sync.dma_start(out[m * P : (m + 1) * P, slots], result[:])

from contextlib import ExitStack

import concourse.mybir as mybir

N, K, T, J = 512, 512, 1024, 512
FLOPS = 2 * N * K * J

F32 = mybir.dt.float32
BF16 = mybir.dt.bfloat16
I32 = mybir.dt.int32
U32 = mybir.dt.uint32
U16 = mybir.dt.uint16
U8 = mybir.dt.uint8
E5M2X4 = mybir.dt.float8_e5m2_x4
E2M1X4 = mybir.dt.float4_e2m1fn_x4
COPY = mybir.ActivationFunctionType.Copy
MULT = mybir.AluOpType.mult
ADD = mybir.AluOpType.add

P = 128
PACK = 4
LAST = PACK - 1
PER_COLUMN = 16
QUADRANT = 32
SCALE_ROWS = 4
HALF = J // 2
PIECE = 128
PIECES = J // PIECE
RUN = 4
BANKS = K // P

PIECE_ORDER = list(range(0, PIECES, 2)) + list(range(1, PIECES, 2))


def tile_list_head_token_grads_kernel(tc, g, gm, w_words, w_scales, base, offs, out):
    nc = tc.nc
    with ExitStack() as ctx:
        keep = ctx.enter_context(tc.tile_pool(name="keep", bufs=1))
        psum = ctx.enter_context(tc.psum_pool(name="psum", bufs=1))

        offsets = keep.tile([P, J // PER_COLUMN], U16, name="offsets")

        warm = keep.tile([P, 2], F32, name="warm")
        nc.vector.memset(warm[:, 0:1], 0.0)
        nc.scalar.activation(warm[:, 1:2], warm[:, 0:1], COPY)

        g_rows = g.rearrange("(p t) c -> p t c", t=PACK)
        planes = []
        for t in range(PACK):
            plane = keep.tile([P, T], F32, name="plane%d" % t)
            nc.sync.dma_start(plane[:], g_rows[:, t, :])
            planes.append(plane)
            if t == 0:
                nc.sync.dma_start(offsets[:], offs)
        factor = keep.tile([P, PACK], F32, name="factor")
        nc.scalar.dma_start(factor[:], gm.rearrange("(p t) o -> p (t o)", t=PACK))

        w_codes = keep.tile([P, 2 * K], U8, name="w_codes", align_bytes=64)
        nc.sync.dma_start(w_codes[:].bitcast(I32), w_words[0].bitcast(I32))
        w_scale_rows = keep.tile([P, K], U8, name="w_scale_rows", align_bytes=64)
        nc.vector.memset(w_scale_rows[:].bitcast(I32), 0)
        for quadrant in range(P // QUADRANT):
            nc.sync.dma_start(
                w_scale_rows[QUADRANT * quadrant : QUADRANT * quadrant + SCALE_ROWS, :].bitcast(I32),
                w_scales[0, SCALE_ROWS * quadrant : SCALE_ROWS * (quadrant + 1), :].bitcast(I32),
            )
        base_rows = keep.tile([P, BANKS, J], F32, name="base_rows")
        nc.sync.dma_start(base_rows[:], base.rearrange("(m p) j -> p m j", p=P))

        last_factor = keep.tile([P, PIECE], F32, name="last_factor")
        nc.scalar.copy(last_factor[:], factor[:, LAST : LAST + 1].to_broadcast([P, PIECE]))

        scaled = [keep.tile([P, PACK, PIECE], F32, name="scaled%d" % q) for q in range(PIECES)]
        for t in range(LAST):
            gathered = HALF if t == LAST - 1 else J
            for first in range(0, J, gathered):
                picked = keep.tile([P, gathered], F32, name="picked%d_%d" % (t, first))
                entries = offsets[:, first // PER_COLUMN : (first + gathered) // PER_COLUMN]
                nc.vector.tensor_copy(picked[:], planes[t][:].indirect(entries))
                for c in range(0, gathered, PIECE):
                    nc.scalar.activation(
                        scaled[(first + c) // PIECE][:, t, :], picked[:, c : c + PIECE], COPY, scale=factor[:, t : t + 1]
                    )
        for q in PIECE_ORDER:
            entries = offsets[:, q * PIECE // PER_COLUMN : (q + 1) * PIECE // PER_COLUMN]
            nc.vector.tensor_tensor(scaled[q][:, LAST, :], planes[LAST][:].indirect(entries), last_factor[:], MULT)

        d_codes = keep.tile([P, J], U32, name="d_codes", align_bytes=64)
        d_scale_rows = keep.tile([P, J], U8, name="d_scale_rows", align_bytes=64)
        woven = [keep.tile([P, PACK * HALF], BF16, name="woven%d" % h, align_bytes=64) for h in range(2)]
        for q in PIECE_ORDER:
            h, odd = divmod(q, 2)
            weave = nc.vector.tensor_copy if odd else nc.scalar.copy
            weave(
                woven[h][:, PACK * PIECE * odd : PACK * PIECE * (odd + 1)].rearrange("p (c i t) -> p c t i", i=RUN, t=PACK),
                scaled[q][:].rearrange("p t (c i) -> p c t i", i=RUN),
            )
        for h in range(2):
            slots = slice(h * HALF, (h + 1) * HALF)
            nc.vector.quantize_mx(out=d_codes[:, slots].bitcast(E5M2X4), scales=d_scale_rows[:, slots], in_=woven[h][:])

        for m in range(BANKS):
            acc = psum.tile([P, J], F32, name="acc%d" % m)
            nc.tensor.matmul_mx(
                out=acc[:],
                lhsT=w_codes[:, 2 * P * m : 2 * P * (m + 1)].bitcast(E2M1X4),
                lhsT_scale=w_scale_rows[:, P * m : P * (m + 1)],
                rhs=d_codes[:].bitcast(E5M2X4),
                rhs_scale=d_scale_rows[:],
                start=True,
                stop=True,
            )
            stored = HALF if m == BANKS - 1 else J
            for first in range(0, J, stored):
                slots = slice(first, first + stored)
                result = keep.tile([P, stored], F32, name="result%d_%d" % (m, first))
                nc.vector.scalar_tensor_tensor(result[:], base_rows[:, m, slots], 0.5, acc[:, slots], MULT, ADD)
                nc.sync.dma_start(out[m * P : (m + 1) * P, slots], result[:])
